import numpy as np
import ml_dtypes


def mxq(x, axis, fmt="e4m3"):
    dtype, down = {"e4m3": (ml_dtypes.float8_e4m3fn, 7), "e5m2": (ml_dtypes.float8_e5m2, 14)}[fmt]
    v = np.moveaxis(np.asarray(x, np.float32).astype(ml_dtypes.bfloat16).astype(np.float64), axis, -1)
    blocks = v.reshape(v.shape[:-1] + (-1, 32))
    amax = np.abs(blocks).max(-1, keepdims=True)
    byte = np.maximum(np.where(amax > 0, np.frexp(amax)[1] - 1 + 127, 0) - down, 1)
    scale = np.exp2(byte - 127.0)
    codes = (blocks / scale).astype(np.float32).astype(dtype).astype(np.float64)
    return np.moveaxis((codes * scale).reshape(v.shape), -1, axis)


WIDE = False


def mx_kscale(k):
    if not WIDE:
        return np.ones(k)
    levels = np.array([10, -10, 5, -5, 0])
    if k % 512:
        return np.exp2(np.random.permutation(np.resize(levels, k // 32))).repeat(32)
    a = np.empty((k // 512, 16))
    for p in range(k // 512):
        a[p, :8] = np.random.permutation(np.resize(levels, 8))
        for g in range(8):
            far = levels[np.abs(levels - a[p, g]) >= 10]
            a[p, g + 8] = far[np.random.randint(len(far))]
    return np.exp2(a.ravel()).repeat(32)


BF16 = ml_dtypes.bfloat16


def bf(x):
    return np.asarray(x, np.float32).astype(BF16)


def f64(x):
    return np.asarray(x).astype(np.float64)


B, P, C, O, R = 2, 1024, 1024, 1024, 768

SLOPE = 0.2
GAIN = float(np.sqrt(2.0))


def lrelu(v):
    return GAIN * np.maximum(v, SLOPE * v)


def setup_inputs():
    s, u = mx_kscale(C), mx_kscale(P)
    return {"x": bf(np.random.standard_normal((B, P, C)) * u[:, None]),
            "style": bf((1.0 + 0.5 * np.random.standard_normal((B, C))) * s),
            "w": bf(np.random.standard_normal((C, O)) / np.sqrt(C) / s[:, None]),
            "noise": bf(np.random.standard_normal((B, P)) * u),
            "strength": bf(0.3 * np.random.standard_normal(O)),
            "g": bf(np.random.standard_normal((B, P, R)) / np.sqrt(P) / u[:, None]),
            "rgb_style": bf(1.0 + 0.5 * np.random.standard_normal((B, O))),
            "rgb_w": bf(np.random.standard_normal((O, R)) / np.sqrt(O))}


def reference(x, style, w, noise, strength, g, rgb_style, rgb_w):
    x, style, w, noise, strength = f64(x), f64(style), f64(w), f64(noise), f64(strength)
    rgb_style, rgb_w = f64(rgb_style), f64(rgb_w)
    demod = 1.0 / np.sqrt(np.sum((style[:, :, None] * w) ** 2, axis=1))
    xs = x * style[:, None, :]
    conv = mxq(xs, 2, "e4m3") @ mxq(w, 0, "e4m3")
    y = lrelu(conv * demod[:, None, :] + noise[:, :, None] * strength)
    d = mxq(y, 1, "e4m3").swapaxes(1, 2) @ mxq(f64(g), 1, "e4m3")
    grad_w = np.sum(rgb_style[:, :, None] * d, axis=0)
    grad_style = np.sum(d * rgb_w, axis=2)
    return grad_w, grad_style

from contextlib import ExitStack
import math

import concourse.mybir as mybir
from concourse.masks import make_identity

B, P, C, O, R = 2, 1024, 1024, 1024, 768
SLOPE = 0.2
GAIN = math.sqrt(2.0)
FLOPS = 2 * B * P * C * O + 2 * B * P * O * R

F32 = mybir.dt.float32
BF16 = mybir.dt.bfloat16
U32 = mybir.dt.uint32
U8 = mybir.dt.uint8
FP8X4 = mybir.dt.float8_e4m3fn_x4
ALU = mybir.AluOpType
ACT = mybir.ActivationFunctionType
AX = mybir.AxisListType

NP = 128
NOT = O // NP
NG = 2
STEPS = B * NOT
CVB = 3
YTB = 3


def tile_modconv_torgb_grads_f4_kernel(
    tc, x, style, w, noise, strength, g, rgb_style, rgb_w, grad_w, grad_style
):
    nc = tc.nc
    with ExitStack() as ctx:
        keep = ctx.enter_context(tc.tile_pool(name="keep", bufs=1))
        work = ctx.enter_context(tc.tile_pool(name="work", bufs=2))
        psum = ctx.enter_context(tc.psum_pool(name="psum", bufs=1))
        ctx.enter_context(tc.manual_schedule())

        ident = keep.tile([NP, NP], F32, name="ident")
        identb = keep.tile([NP, NP], BF16, name="identb")
        rows = keep.tile([NP, 512], BF16, name="rows")
        nz = keep.tile([NP, B * NG, NP], BF16, name="nz")
        nlt = keep.tile([NP, B * NG, NP], BF16, name="nlt")
        srow = keep.tile([NP, NOT, 4, NP], BF16, name="srow")
        rs = keep.tile([NP, B * NOT], F32, name="rs")
        st4 = keep.tile([NP, B * 2, 4], BF16, name="st4")
        s2 = keep.tile([NP, 2, 4, B], F32, name="s2")
        dm = keep.tile([NP, NOT, B], F32, name="dm")
        sd = keep.tile([NP, NOT, B], F32, name="sd")
        gsp = keep.tile([NP, STEPS, 2], F32, name="gsp")
        gsum = keep.tile([NP, NP], F32, name="gsum")
        gout = keep.tile([16, NP], F32, name="gout")
        dmy = keep.tile([NP, 1], F32, name="dmy")
        wa = keep.tile([NP, 2, 4, 256], BF16, name="wa")
        wb = keep.tile([NP, 2, 4, 768], BF16, name="wb")
        xraw, graw, xc, xs, gc, gsc = {}, {}, {}, {}, {}, {}
        for b in range(B):
            for q in range(NG):
                for u in range(2):
                    xr = work.tile([NP, 2, C], BF16, name="xr", tag="xr", bufs=6)
                    xraw[b, q, u] = xr
                gr = work.tile([NP, 4, R], BF16, name="gr", tag="gr", bufs=2)
                graw[b, q] = gr
                xcodes = keep.tile([NP, 2, 512], U32, name="xc%d%d" % (b, q), align_bytes=256)
                xscale = keep.tile([NP, 2, 512], U8, name="xs%d%d" % (b, q), align_bytes=256)
                xc[b, q], xs[b, q] = xcodes, xscale
                gcodes = keep.tile([NP, R], U32, name="gc%d%d" % (b, q), align_bytes=256)
                gscale = keep.tile([NP, R], U8, name="gs%d%d" % (b, q), align_bytes=256)
                gc[b, q], gsc[b, q] = gcodes, gscale
        wc, ws, rw, gw = {}, {}, {}, {}
        for ot in range(NOT):
            wcodes = keep.tile([NP, 2, NP], U32, name="wc%d" % ot, align_bytes=256)
            wscale = keep.tile([NP, 2, NP], U8, name="ws%d" % ot, align_bytes=256)
            wc[ot], ws[ot] = wcodes, wscale
            gwt = keep.tile([NP, R], F32, name="gw%d" % ot)
            gw[ot] = gwt
        for h in range(2):
            rwt = keep.tile([NP, 4, R], BF16, name="rw%d" % h)
            rw[h] = rwt

        make_identity(nc, ident[:])
        nc.vector.memset(rows[:], 0.0)
        nc.vector.memset(dmy[:], 1.0)
        nc.scalar.activation(out=dmy[:], in_=dmy[:], func=ACT.Sqrt)
        nc.vector.memset(nz[:], 0.0)
        nc.vector.tensor_copy(out=identb[:], in_=ident[:])
        nc.vector.memset(srow[:], 0.0)
        nc.gpsimd.memset(gsum[:], 0.0)

        xv = x.rearrange("b (q p u e) c -> b q u p e c", q=NG, p=NP, u=2, e=2)
        wv = w.rearrange("(k p j) o -> k p j o", k=2, p=NP)
        gv = g.rearrange("b (q p t) r -> b q p t r", q=NG, p=NP)
        rwv = rgb_w.rearrange("(h t p) r -> h p t r", h=2, p=NP)

        def load_x(b, q, u):
            nc.sync.dma_start(out=xraw[b, q, u][:], in_=xv[b, q, u])

        nc.sync.dma_start(out=rows[0:4, :], in_=style.rearrange("b (k n) -> (b k) n", n=512))
        nc.sync.dma_start(out=rows[4:8, :], in_=rgb_style.rearrange("b (k n) -> (b k) n", n=512))
        nc.sync.dma_start(out=rows[8:12, :], in_=noise.rearrange("b (k n) -> (b k) n", n=512))
        load_x(0, 0, 0)
        load_x(0, 0, 1)
        for k in range(2):
            nc.sync.dma_start(out=wa[:, k], in_=wv[k, :, :, 0:256])
        load_x(0, 1, 0)
        load_x(0, 1, 1)
        for t in range(4):
            nc.sync.dma_start(
                out=srow[t : t + 1, :, t, :], in_=strength.rearrange("(a h n) -> a h n", a=1, n=NP)
            )
        for k in range(2):
            nc.sync.dma_start(out=wb[:, k], in_=wv[k, :, :, 256:1024])
        for q in range(NG):
            nc.sync.dma_start(out=graw[0, q][:], in_=gv[0, q])
        load_x(1, 0, 0)
        nc.sync.dma_start(out=rw[0][:], in_=rwv[0])
        load_x(1, 0, 1)
        load_x(1, 1, 0)
        load_x(1, 1, 1)
        nc.sync.dma_start(out=rw[1][:], in_=rwv[1])
        for q in range(NG):
            nc.sync.dma_start(out=graw[1, q][:], in_=gv[1, q])

        pst = psum.tile([NP, 4, NP], BF16, name="cv", tag="cv", bufs=CVB)
        for j in range(4):
            nc.tensor.transpose(pst[:, j, :], rows[:, j:512:4], identb[:])
        nc.vector.tensor_copy(out=st4[:], in_=pst[:, :, 0:4].rearrange("p j n -> p n j"))
        nc.vector.tensor_copy(out=nz[:, :, 0:4], in_=pst[:, :, 8:12].rearrange("p j n -> p n j"))
        for b in range(B):
            nc.vector.tensor_tensor(
                out=s2[:, :, :, b], in0=st4[:, 2 * b : 2 * b + 2, :], in1=st4[:, 2 * b : 2 * b + 2, :], op=ALU.mult
            )

        def small_rows():
            pz = psum.tile([NP, B * NG, NP], BF16, name="cv", tag="cv", bufs=CVB)
            for i in range(B * NG):
                nc.tensor.transpose(pz[:, i, :], nz[:, i, :], identb[:])
            nc.scalar.copy(out=nlt[:], in_=pz[:])
            psr = psum.tile([NP, 4, NP], BF16, name="cv", tag="cv", bufs=CVB)
            for c in range(4):
                nc.tensor.transpose(psr[:, c, :], rows[:, c * NP : (c + 1) * NP], identb[:])
            nc.scalar.copy(out=rs[:].rearrange("p (k c) -> p k c", c=4), in_=psr[:, :, 4:8].rearrange("p c k -> p k c"))

        live = {}

        def x_turn(b, q, u, k):
            xt = psum.tile([NP, 2, 2, NP], F32, name="cv", tag="cv", bufs=CVB)
            live["xt", b, q, u, k] = xt
            for e in range(2):
                words = xraw[b, q, u][:, e, :].bitcast(F32)
                for h in range(2):
                    nc.tensor.transpose(xt[:, h, e, :], words[:, 256 * k + h : 256 * (k + 1) : 2], ident[:])

        def x_style(b, q, u, k):
            xt = live["xt", b, q, u, k]
            if ("xi", b, q, k) not in live:
                xi = work.tile([NP, 2, 256, 4], BF16, name="xi", tag="xi", bufs=4, align_bytes=256)
                live["xi", b, q, k] = xi
            xi = live["xi", b, q, k]
            nc.vector.tensor_tensor(
                out=xi[:, u].rearrange("p n (h f) -> p n h f", f=2),
                in0=xt[:].rearrange("p h e r -> p (h e r)").bitcast(BF16).rearrange("p (h n f) -> p n h f", h=2, f=2),
                in1=st4[:, 2 * b + k].rearrange("p (h f) -> p h f", f=2).unsqueeze(1).to_broadcast([NP, 256, 2, 2]),
                op=ALU.mult,
            )

        def x_quant(b, q, k):
            nc.vector.quantize_mx(
                out=xc[b, q][:, k].bitcast(FP8X4),
                scales=xs[b, q][:, k],
                in_=live["xi", b, q, k][:].rearrange("p u n t -> p (u n t)"),
            )

        def w_cols(ot):
            if ot < 2:
                return wa[:, :, :, ot * NP : (ot + 1) * NP]
            return wb[:, :, :, (ot - 2) * NP : (ot - 1) * NP]

        def copy_on(eng, out, in_):
            if eng == 0:
                nc.scalar.copy(out=out, in_=in_)
            else:
                nc.vector.tensor_copy(out=out, in_=in_)

        def w_il(ot, eng):
            wi = work.tile([NP, 2, NP, 4], BF16, name="wi", tag="wi", bufs=2, align_bytes=256)
            live["wi", ot] = wi
            copy_on(eng, wi[:], w_cols(ot).rearrange("p k j o -> p k o j"))

        def w_sq(ot):
            sq = work.tile([NP, 2, 4, NP], F32, name="sq", tag="sq", bufs=2)
            live["sq", ot] = sq
            nc.scalar.activation(out=sq[:], in_=w_cols(ot), func=ACT.Square)

        def w_quant(ot):
            nc.vector.quantize_mx(
                out=wc[ot][:].rearrange("p k o -> p (k o)").bitcast(FP8X4),
                scales=ws[ot][:].rearrange("p k o -> p (k o)"),
                in_=live["wi", ot][:].rearrange("p k o j -> p (k o j)"),
            )

        def demod(ot):
            pd = psum.tile([NP, B], F32, name="cv", tag="cv", bufs=CVB)
            live["pd", ot] = pd
            for k in range(2):
                for j in range(4):
                    nc.tensor.matmul(
                        pd[:],
                        lhsT=live["sq", ot][:, k, j, :],
                        rhs=s2[:, k, j, :],
                        start=(k == 0 and j == 0),
                        stop=(k == 1 and j == 3),
                    )

        def demod_root(ot):
            nc.scalar.activation(out=sd[:, ot, :], in_=live["pd", ot][:], func=ACT.Sqrt)

        def demod_inv(ot):
            nc.vector.reciprocal(out=dm[:, ot, :], in_=sd[:, ot, :])

        PIECES = ((0, 512), (512, R))

        def g_il(b, q, i, eng):
            if ("gi", b, q) not in live:
                gi = work.tile([NP, R, 4], BF16, name="gi", tag="gi", bufs=2, align_bytes=256)
                live["gi", b, q] = gi
            lo, hi = PIECES[i]
            copy_on(eng, live["gi", b, q][:, lo:hi, :], graw[b, q][:, :, lo:hi].rearrange("p t r -> p r t"))

        def g_quant(b, q, i):
            lo, hi = PIECES[i]
            nc.vector.quantize_mx(
                out=gc[b, q][:, lo:hi].bitcast(FP8X4),
                scales=gsc[b, q][:, lo:hi],
                in_=live["gi", b, q][:, lo:hi, :].rearrange("p r t -> p (r t)"),
            )

        def conv(s, q):
            b, ot = divmod(s, NOT)
            cv = psum.tile([NP, 512], F32, name="cv", tag="cv", bufs=CVB)
            live["cv", s, q] = cv
            for k in range(2):
                nc.tensor.matmul_mx(
                    out=cv[:],
                    lhsT=wc[ot][:, k].bitcast(FP8X4),
                    lhsT_scale=ws[ot][:, k],
                    rhs=xc[b, q][:, k].bitcast(FP8X4),
                    rhs_scale=xs[b, q][:, k],
                    start=(k == 0),
                    stop=(k == 1),
                )

        def scale(s, q):
            b, ot = divmod(s, NOT)
            if ("vt", s) not in live:
                vt = work.tile([NP, P], F32, name="vt", tag="vt", bufs=3)
                live["vt", s] = vt
            nc.scalar.activation(
                out=live["vt", s][:, q * 512 : (q + 1) * 512],
                in_=live["cv", s, q][:],
                func=ACT.Copy,
                scale=dm[:, ot, b : b + 1],
            )

        def noise_mm(s, q):
            b, ot = divmod(s, NOT)
            yt = psum.tile([NP, 4, NP], F32, name="yt", tag="yt", bufs=YTB)
            live["yt", s, q] = yt
            nc.tensor.matmul(
                yt[:].rearrange("p t o -> p (t o)"),
                lhsT=nlt[:, b * NG + q, :],
                rhs=srow[:, ot].rearrange("p t o -> p (t o)"),
                start=True,
                stop=False,
            )

        def turn(s, q):
            for t in range(4):
                lo = q * 512 + t * NP
                nc.tensor.matmul(
                    live["yt", s, q][:, t, :],
                    lhsT=live["vt", s][:, lo : lo + NP],
                    rhs=ident[:],
                    start=False,
                    stop=(t == 3),
                    is_transpose=True,
                )

        def slope(s, q):
            if ("vn", s) not in live:
                vn = work.tile([NP, 2, NP, 4], F32, name="vn", tag="vn", bufs=2)
                live["vn", s] = vn
            nc.scalar.activation(
                out=live["vn", s][:, q],
                in_=live["yt", s, q][:].rearrange("p t o -> p o t"),
                func=ACT.Copy,
                scale=SLOPE * GAIN,
            )

        def leaky(s, q):
            if ("yi", s) not in live:
                yi = work.tile([NP, 2, NP, 4], BF16, name="yi", tag="yi", bufs=2, align_bytes=256)
                live["yi", s] = yi
            nc.vector.scalar_tensor_tensor(
                out=live["yi", s][:, q],
                in0=live["yt", s, q][:].rearrange("p t o -> p o t"),
                scalar=GAIN,
                in1=live["vn", s][:, q],
                op0=ALU.mult,
                op1=ALU.max,
            )

        def y_quant(s):
            yc = work.tile([NP, 2, NP], U32, name="yc", tag="yc", bufs=2, align_bytes=256)
            ys = work.tile([NP, 2, NP], U8, name="ys", tag="ys", bufs=2, align_bytes=256)
            live["yc", s] = (yc, ys)
            nc.vector.quantize_mx(
                out=yc[:].rearrange("p q o -> p (q o)").bitcast(FP8X4),
                scales=ys[:].rearrange("p q o -> p (q o)"),
                in_=live["yi", s][:].rearrange("p q o t -> p (q o t)"),
            )

        def d_mm(s, i):
            b, ot = divmod(s, NOT)
            yc, ys = live["yc", s]
            lo, hi = PIECES[i]
            if i == 0:
                da = psum.tile([NP, 512], F32, name="da", tag="da", bufs=1)
                live["d", s, 0] = da
            else:
                db = psum.tile([NP, 256], F32, name="db", tag="db", bufs=1)
                live["d", s, 1] = db
            for q in range(NG):
                nc.tensor.matmul_mx(
                    out=live["d", s, i][:],
                    lhsT=yc[:, q].bitcast(FP8X4),
                    lhsT_scale=ys[:, q],
                    rhs=gc[b, q][:, lo:hi].bitcast(FP8X4),
                    rhs_scale=gsc[b, q][:, lo:hi],
                    start=(q == 0),
                    stop=(q == 1),
                )

        def gs_part(s, i):
            b, ot = divmod(s, NOT)
            lo, hi = PIECES[i]
            junk = work.tile([NP, 512], BF16, name="junk", tag="junk", bufs=1)
            nc.vector.scalar_tensor_tensor(
                out=junk[:, 0 : hi - lo],
                in0=live["d", s, i][:],
                scalar=1.0,
                in1=rw[ot // 4][:, ot % 4, lo:hi],
                op0=ALU.mult,
                op1=ALU.mult,
                accum_out=gsp[:, s, i : i + 1],
            )

        def gw_part(s, i):
            b, ot = divmod(s, NOT)
            lo, hi = PIECES[i]
            if b == 0:
                nc.scalar.activation(
                    out=gw[ot][:, lo:hi], in_=live["d", s, i][:], func=ACT.Copy, scale=rs[:, s : s + 1]
                )
                return
            if ("go", s) not in live:
                go = work.tile([NP, R], F32, name="go", tag="go", bufs=2)
                live["go", s] = go
            nc.vector.scalar_tensor_tensor(
                out=live["go", s][:, lo:hi],
                in0=live["d", s, i][:],
                scalar=rs[:, s : s + 1],
                in1=gw[ot][:, lo:hi],
                op0=ALU.mult,
                op1=ALU.add,
            )
            nc.sync.dma_start(out=grad_w[ot * NP : (ot + 1) * NP, lo:hi], in_=live["go", s][:, lo:hi])

        order = (
            (small_rows,),
            (x_turn, 0, 0, 0, 0),
            (x_turn, 0, 0, 0, 1),
            (x_style, 0, 0, 0, 0),
            (x_turn, 0, 0, 1, 0),
            (x_style, 0, 0, 0, 1),
            (x_turn, 0, 0, 1, 1),
            (x_style, 0, 0, 1, 0),
            (w_sq, 0,),
            (x_style, 0, 0, 1, 1),
            (x_quant, 0, 0, 0),
            (w_sq, 1,),
            (x_turn, 0, 1, 0, 0),
            (x_quant, 0, 0, 1),
            (x_turn, 0, 1, 0, 1),
            (x_style, 0, 1, 0, 0),
            (w_il, 0, 0),
            (x_turn, 0, 1, 1, 0),
            (x_style, 0, 1, 0, 1),
            (x_turn, 0, 1, 1, 1),
            (x_style, 0, 1, 1, 0),
            (demod, 0,),
            (w_il, 1, 0),
            (x_style, 0, 1, 1, 1),
            (x_quant, 0, 1, 0),
            (demod, 1,),
            (x_quant, 0, 1, 1),
            (demod_root, 0,),
            (w_quant, 0,),
            (noise_mm, 0, 0),
            (demod_inv, 0,),
            (w_quant, 1,),
            (conv, 0, 0),
            (demod_root, 1,),
            (demod_inv, 1,),
            (w_sq, 2,),
            (conv, 0, 1),
            (noise_mm, 0, 1),
            (noise_mm, 1, 0),
            (w_sq, 3,),
            (demod, 2,),
            (g_il, 0, 0, 0, 1),
            (scale, 0, 0),
            (scale, 0, 1),
            (turn, 0, 0),
            (g_il, 0, 0, 1, 1),
            (demod_root, 2,),
            (w_sq, 4,),
            (conv, 1, 0),
            (g_il, 0, 1, 0, 1),
            (turn, 0, 1),
            (w_il, 2, 0),
            (conv, 1, 1),
            (g_il, 0, 1, 1, 1),
            (demod, 3,),
            (scale, 1, 0),
            (g_quant, 0, 0, 0),
            (scale, 1, 1),
            (w_quant, 2,),
            (g_quant, 0, 0, 1),
            (x_turn, 1, 0, 0, 0),
            (demod_root, 3,),
            (w_sq, 5,),
            (demod_inv, 2,),
            (g_quant, 0, 1, 0),
            (x_turn, 1, 0, 0, 1),
            (x_style, 1, 0, 0, 0),
            (turn, 1, 0),
            (slope, 0, 0),
            (x_turn, 1, 0, 1, 0),
            (x_style, 1, 0, 0, 1),
            (slope, 0, 1),
            (x_turn, 1, 0, 1, 1),
            (demod_inv, 3,),
            (g_quant, 0, 1, 1),
            (x_style, 1, 0, 1, 0),
            (w_il, 3, 0),
            (x_turn, 1, 1, 0, 0),
            (leaky, 0, 0),
            (x_turn, 1, 1, 0, 1),
            (leaky, 0, 1),
            (w_il, 4, 0),
            (noise_mm, 1, 1),
            (x_style, 1, 0, 1, 1),
            (turn, 1, 1),
            (x_style, 1, 1, 0, 0),
            (noise_mm, 2, 0),
            (slope, 1, 0),
            (x_turn, 1, 1, 1, 0),
            (x_style, 1, 1, 0, 1),
            (slope, 1, 1),
            (x_turn, 1, 1, 1, 1),
            (w_quant, 3,),
            (x_style, 1, 1, 1, 0),
            (conv, 2, 0),
            (w_il, 5, 0),
            (x_style, 1, 1, 1, 1),
            (conv, 2, 1),
            (x_quant, 1, 0, 0),
            (demod, 4,),
            (scale, 2, 0),
            (x_quant, 1, 0, 1),
            (scale, 2, 1),
            (x_quant, 1, 1, 0),
            (turn, 2, 0),
            (demod_root, 4,),
            (w_sq, 6,),
            (x_quant, 1, 1, 1),
            (demod, 5,),
            (y_quant, 0,),
            (leaky, 1, 0),
            (slope, 2, 0),
            (conv, 3, 0),
            (leaky, 1, 1),
            (demod_root, 5,),
            (w_sq, 7,),
            (d_mm, 0, 0),
            (w_quant, 4,),
            (demod_inv, 4,),
            (y_quant, 1,),
            (noise_mm, 2, 1),
            (leaky, 2, 0),
            (gw_part, 0, 0),
            (turn, 2, 1),
            (conv, 3, 1),
            (w_quant, 5,),
            (scale, 3, 0),
            (demod_inv, 5,),
            (gs_part, 0, 0),
            (noise_mm, 3, 0),
            (slope, 2, 1),
            (d_mm, 0, 1),
            (g_il, 1, 0, 0, 1),
            (noise_mm, 3, 1),
            (scale, 3, 1),
            (demod, 6,),
            (w_il, 6, 0),
            (leaky, 2, 1),
            (turn, 3, 0),
            (gs_part, 0, 1),
            (turn, 3, 1),
            (demod_root, 6,),
            (w_il, 7, 0),
            (y_quant, 2,),
            (d_mm, 1, 0),
            (w_quant, 6,),
            (g_quant, 1, 0, 0),
            (conv, 4, 0),
            (slope, 3, 0),
            (demod_inv, 6,),
            (conv, 4, 1),
            (gs_part, 1, 0),
            (slope, 3, 1),
            (demod, 7,),
            (w_quant, 7,),
            (leaky, 3, 0),
            (scale, 4, 0),
            (leaky, 3, 1),
            (scale, 4, 1),
            (noise_mm, 4, 0),
            (turn, 4, 0),
            (g_il, 1, 0, 1, 1),
            (demod_root, 7,),
            (gw_part, 0, 1),
            (noise_mm, 4, 1),
            (gw_part, 1, 0),
            (demod_inv, 7,),
            (g_il, 1, 1, 0, 1),
            (turn, 4, 1),
            (slope, 4, 0),
            (d_mm, 1, 1),
            (d_mm, 2, 0),
            (slope, 4, 1),
            (gs_part, 1, 1),
            (conv, 5, 0),
            (gw_part, 1, 1),
            (y_quant, 3,),
            (gw_part, 2, 0),
            (conv, 5, 1),
            (leaky, 4, 0),
            (scale, 5, 0),
            (noise_mm, 5, 0),
            (leaky, 4, 1),
            (d_mm, 2, 1),
            (scale, 5, 1),
            (noise_mm, 5, 1),
            (g_quant, 1, 0, 1),
            (conv, 6, 0),
            (gs_part, 2, 0),
            (gw_part, 2, 1),
            (turn, 5, 0),
            (y_quant, 4,),
            (scale, 6, 0),
            (turn, 5, 1),
            (gs_part, 2, 1),
            (slope, 5, 0),
            (g_il, 1, 1, 1, 1),
            (d_mm, 3, 0),
            (slope, 5, 1),
            (conv, 6, 1),
            (g_quant, 1, 1, 0),
            (noise_mm, 6, 0),
            (gw_part, 3, 0),
            (leaky, 5, 0),
            (d_mm, 3, 1),
            (conv, 7, 0),
            (scale, 6, 1),
            (leaky, 5, 1),
            (noise_mm, 6, 1),
            (gw_part, 3, 1),
            (gs_part, 3, 0),
            (turn, 6, 0),
            (scale, 7, 0),
            (turn, 6, 1),
            (y_quant, 5,),
            (slope, 6, 0),
            (gs_part, 3, 1),
            (conv, 7, 1),
            (g_quant, 1, 1, 1),
            (slope, 6, 1),
            (d_mm, 4, 0),
            (leaky, 6, 0),
            (scale, 7, 1),
            (noise_mm, 7, 0),
            (leaky, 6, 1),
            (d_mm, 4, 1),
            (gw_part, 4, 0),
            (turn, 7, 0),
            (gs_part, 4, 0),
            (gw_part, 4, 1),
            (conv, 8, 0),
            (y_quant, 6,),
            (slope, 7, 0),
            (gs_part, 4, 1),
            (noise_mm, 7, 1),
            (scale, 8, 0),
            (turn, 7, 1),
            (leaky, 7, 0),
            (d_mm, 5, 0),
            (slope, 7, 1),
            (conv, 8, 1),
            (gs_part, 5, 0),
            (gw_part, 5, 0),
            (noise_mm, 8, 0),
            (d_mm, 5, 1),
            (scale, 8, 1),
            (leaky, 7, 1),
            (noise_mm, 8, 1),
            (d_mm, 6, 0),
            (gw_part, 5, 1),
            (gs_part, 5, 1),
            (y_quant, 7,),
            (turn, 8, 0),
            (gs_part, 6, 0),
            (gw_part, 6, 0),
            (turn, 8, 1),
            (slope, 8, 0),
            (conv, 9, 0),
            (slope, 8, 1),
            (conv, 9, 1),
            (leaky, 8, 0),
            (noise_mm, 9, 0),
            (scale, 9, 0),
            (d_mm, 6, 1),
            (leaky, 8, 1),
            (d_mm, 7, 0),
            (scale, 9, 1),
            (gs_part, 6, 1),
            (noise_mm, 9, 1),
            (gw_part, 6, 1),
            (y_quant, 8,),
            (turn, 9, 0),
            (gw_part, 7, 0),
            (gs_part, 7, 0),
            (turn, 9, 1),
            (slope, 9, 0),
            (conv, 10, 0),
            (slope, 9, 1),
            (conv, 10, 1),
            (leaky, 9, 0),
            (scale, 10, 0),
            (noise_mm, 10, 0),
            (leaky, 9, 1),
            (d_mm, 7, 1),
            (scale, 10, 1),
            (noise_mm, 10, 1),
            (gs_part, 7, 1),
            (turn, 10, 0),
            (gw_part, 7, 1),
            (y_quant, 9,),
            (d_mm, 8, 0),
            (slope, 10, 0),
            (turn, 10, 1),
            (gw_part, 8, 0),
            (conv, 11, 0),
            (slope, 10, 1),
            (leaky, 10, 0),
            (conv, 11, 1),
            (scale, 11, 0),
            (gs_part, 8, 0),
            (noise_mm, 11, 0),
            (d_mm, 8, 1),
            (scale, 11, 1),
            (leaky, 10, 1),
            (noise_mm, 11, 1),
            (gw_part, 8, 1),
            (turn, 11, 0),
            (gs_part, 8, 1),
            (turn, 11, 1),
            (slope, 11, 0),
            (y_quant, 10,),
            (d_mm, 9, 0),
            (slope, 11, 1),
            (conv, 12, 0),
            (leaky, 11, 0),
            (conv, 12, 1),
            (leaky, 11, 1),
            (scale, 12, 0),
            (noise_mm, 12, 0),
            (gw_part, 9, 0),
            (d_mm, 9, 1),
            (scale, 12, 1),
            (noise_mm, 12, 1),
            (gs_part, 9, 0),
            (turn, 12, 0),
            (turn, 12, 1),
            (gw_part, 9, 1),
            (slope, 12, 0),
            (gs_part, 9, 1),
            (conv, 13, 0),
            (y_quant, 11,),
            (slope, 12, 1),
            (d_mm, 10, 0),
            (leaky, 12, 0),
            (scale, 13, 0),
            (conv, 13, 1),
            (leaky, 12, 1),
            (noise_mm, 13, 0),
            (gw_part, 10, 0),
            (d_mm, 10, 1),
            (scale, 13, 1),
            (noise_mm, 13, 1),
            (gs_part, 10, 0),
            (turn, 13, 0),
            (turn, 13, 1),
            (gw_part, 10, 1),
            (slope, 13, 0),
            (gs_part, 10, 1),
            (conv, 14, 0),
            (y_quant, 12,),
            (slope, 13, 1),
            (d_mm, 11, 0),
            (leaky, 13, 0),
            (scale, 14, 0),
            (conv, 14, 1),
            (leaky, 13, 1),
            (noise_mm, 14, 0),
            (gw_part, 11, 0),
            (d_mm, 11, 1),
            (scale, 14, 1),
            (noise_mm, 14, 1),
            (gs_part, 11, 0),
            (turn, 14, 0),
            (turn, 14, 1),
            (gw_part, 11, 1),
            (slope, 14, 0),
            (gs_part, 11, 1),
            (conv, 15, 0),
            (y_quant, 13,),
            (slope, 14, 1),
            (d_mm, 12, 0),
            (leaky, 14, 0),
            (scale, 15, 0),
            (conv, 15, 1),
            (leaky, 14, 1),
            (noise_mm, 15, 0),
            (gw_part, 12, 0),
            (d_mm, 12, 1),
            (scale, 15, 1),
            (noise_mm, 15, 1),
            (gs_part, 12, 0),
            (turn, 15, 0),
            (turn, 15, 1),
            (gw_part, 12, 1),
            (slope, 15, 0),
            (gs_part, 12, 1),
            (d_mm, 13, 0),
            (y_quant, 14,),
            (slope, 15, 1),
            (d_mm, 13, 1),
            (leaky, 15, 0),
            (leaky, 15, 1),
            (gw_part, 13, 0),
            (gs_part, 13, 0),
            (gw_part, 13, 1),
            (d_mm, 14, 0),
            (gs_part, 13, 1),
            (y_quant, 15,),
            (d_mm, 14, 1),
            (gw_part, 14, 0),
            (gs_part, 14, 0),
            (gw_part, 14, 1),
            (d_mm, 15, 0),
            (gs_part, 14, 1),
            (d_mm, 15, 1),
            (gs_part, 15, 0),
            (gw_part, 15, 0),
            (gs_part, 15, 1),
            (gw_part, 15, 1),
        )
        for fn, *args in order:
            fn(*args)

        nc.vector.tensor_reduce(out=gsum[:, 0:STEPS], in_=gsp[:], axis=AX.X, op=ALU.add)
        pg = psum.tile([NP, NP], F32, name="cv", tag="cv", bufs=CVB)
        nc.tensor.transpose(pg[:], gsum[:], ident[:])
        nc.scalar.copy(out=gout[:], in_=pg[0:STEPS, :])
        nc.sync.dma_start(out=grad_style.rearrange("b (t p) -> (b t) p", p=NP), in_=gout[:])
